import numpy as np
import ml_dtypes

BF16 = ml_dtypes.bfloat16


def bf(x):
    return np.asarray(x, np.float32).astype(BF16)


def f32(x):
    return np.asarray(x, np.float32)


def f64(x):
    return np.asarray(x).astype(np.float64)


def striped(idx):
    return np.tile(idx.reshape(-1, 16).T, (8, 1))


S, K, M, N, E, Q = 512, 128, 384, 512, 4, 128


def setup_inputs():
    return {"base": bf(np.random.standard_normal((M, S))), "x": bf(np.random.standard_normal((K, N))), "w": bf(1.2 * np.random.standard_normal((E, K, M)) / np.sqrt(K)), "s": f32(0.5 + np.random.random_sample((M, 1))), "offs": striped(np.random.permutation(S))}


def reference(base, x, w, s, offs):
    idx = offs[:16].T.reshape(-1)
    z = f64(base).copy()
    for e in range(E):
        z[:, idx[e * Q : (e + 1) * Q]] += f64(w)[e].T @ f64(x)[:, e * Q : (e + 1) * Q]
    z = z / np.sqrt((z**2).mean(axis=0, keepdims=True) + 1e-5) * f64(s)
    return z

@@ -1,0 +1,84 @@
+import concourse.mybir as mybir
+from concourse.masks import make_identity
+
+BF16, F32, U16 = mybir.dt.bfloat16, mybir.dt.float32, mybir.dt.uint16
+MULT = mybir.AluOpType.mult
+ABS_RSQRT = mybir.ActivationFunctionType.Abs_reciprocal_sqrt
+SQUARE = mybir.ActivationFunctionType.Square
+
+P = 128
+EPS = 1e-5
+FLOPS = 2 * 128 * 384 * 512
+
+
+def tile_rows_placenorm_base_kernel(tc, base, x, w, s, offs, out):
+    nc = tc.nc
+    features, tokens = base.shape
+    experts = w.shape[0]
+    blocks = features // P
+    entries = x.shape[1] // experts
+    piece = entries // 16
+    half = tokens // 2
+
+    with (
+        tc.tile_pool(name="held", bufs=1) as held,
+        tc.psum_pool(name="psum", bufs=1) as psum,
+    ):
+        base_tile = held.tile([P, blocks, tokens], BF16, name="base_tile")
+        nc.sync.dma_start(base_tile[:], base.rearrange("(a p) n -> p a n", p=P))
+        w_tile = held.tile([P, experts, features], BF16, name="w_tile")
+        nc.scalar.dma_start(w_tile[:], w.rearrange("e k m -> k e m"))
+        x_tile = held.tile([P, experts * entries], BF16, name="x_tile")
+        nc.sync.dma_start(x_tile[:], x)
+        offsets = held.tile([P, experts * piece], U16, name="offsets")
+        nc.sync.dma_start(offsets[:], offs)
+        gain = held.tile([P, blocks], F32, name="gain")
+        nc.sync.dma_start(gain[:], s.rearrange("(a p) o -> p (a o)", p=P))
+
+        identity = held.tile([P, P], BF16, name="identity")
+        make_identity(nc, identity[:])
+        ones = held.tile([P, P], BF16, name="ones")
+        nc.vector.memset(ones[:], 1.0)
+        eps = held.tile([P, 1], F32, name="eps")
+        nc.vector.memset(eps[:], EPS)
+
+        early = held.tile([P, 1], F32, name="early")
+        nc.scalar.activation(early[:], eps[:], ABS_RSQRT, bias=eps[:])
+
+        windows = [psum.tile([P, tokens], F32, name=f"window{a}") for a in range(blocks)]
+        for a in range(blocks):
+            nc.tensor.matmul(windows[a][:], identity[:], base_tile[:, a, :], start=True, stop=False)
+
+        for a in range(blocks):
+            for e in range(experts):
+                nc.tensor.matmul(
+                    windows[a][:].indirect(offsets[:, e * piece : (e + 1) * piece]),
+                    w_tile[:, e, a * P : (a + 1) * P],
+                    x_tile[:, e * entries : (e + 1) * entries],
+                    start=False,
+                    stop=e == experts - 1,
+                )
+
+        squares = [held.tile([P, tokens], BF16, name=f"squares{a}") for a in range(blocks)]
+        for a in range(blocks - 1):
+            nc.scalar.activation(squares[a][:], windows[a][:], SQUARE)
+        for h in range(2):
+            cols = slice(h * half, (h + 1) * half)
+            nc.scalar.activation(squares[-1][:, cols], windows[-1][:, cols], SQUARE)
+
+        sums = [psum.tile([P, half], F32, name=f"sums{h}") for h in range(2)]
+        for h in range(2):
+            cols = slice(h * half, (h + 1) * half)
+            for a in range(blocks):
+                nc.tensor.matmul(sums[h][:], ones[:], squares[a][:, cols], start=a == 0, stop=a == blocks - 1)
+
+        for h in range(2):
+            cols = slice(h * half, (h + 1) * half)
+            rnorm = held.tile([P, half], F32, name=f"rnorm{h}")
+            nc.scalar.activation(rnorm[:], sums[h][:], ABS_RSQRT, bias=eps[:], scale=1.0 / features)
+            for a in range(blocks):
+                normed = held.tile([P, half], F32, name=f"normed{h}_{a}")
+                nc.vector.scalar_tensor_tensor(
+                    normed[:], windows[a][:, cols], gain[:, a : a + 1], rnorm[:], op0=MULT, op1=MULT
+                )
+                nc.sync.dma_start(out[a * P : (a + 1) * P, cols], normed[:])

@@ -19,6 +19,7 @@ def tile_rows_placenorm_base_kernel(tc, base, x, w, s, offs, out):
     entries = x.shape[1] // experts
     piece = entries // 16
     half = tokens // 2
+    warmups = 4
 
     with (
         tc.tile_pool(name="held", bufs=1) as held,
@@ -34,6 +35,12 @@ def tile_rows_placenorm_base_kernel(tc, base, x, w, s, offs, out):
         nc.sync.dma_start(offsets[:], offs)
         gain = held.tile([P, blocks], F32, name="gain")
         nc.sync.dma_start(gain[:], s.rearrange("(a p) o -> p (a o)", p=P))
+
+        zeros = held.tile([P, tokens], BF16, name="zeros")
+        nc.vector.memset(zeros[:], 0.0)
+        spare = psum.tile([P, tokens], F32, name="spare")
+        for warmup in range(warmups):
+            nc.tensor.matmul(spare[:], zeros[:, :P], zeros[:], start=True, stop=True)
 
         identity = held.tile([P, P], BF16, name="identity")
         make_identity(nc, identity[:])

@@ -19,7 +19,7 @@ def tile_rows_placenorm_base_kernel(tc, base, x, w, s, offs, out):
     entries = x.shape[1] // experts
     piece = entries // 16
     half = tokens // 2
-    warmups = 4
+    warmups = 3
 
     with (
         tc.tile_pool(name="held", bufs=1) as held,
@@ -27,12 +27,12 @@ def tile_rows_placenorm_base_kernel(tc, base, x, w, s, offs, out):
     ):
         base_tile = held.tile([P, blocks, tokens], BF16, name="base_tile")
         nc.sync.dma_start(base_tile[:], base.rearrange("(a p) n -> p a n", p=P))
-        w_tile = held.tile([P, experts, features], BF16, name="w_tile")
-        nc.scalar.dma_start(w_tile[:], w.rearrange("e k m -> k e m"))
-        x_tile = held.tile([P, experts * entries], BF16, name="x_tile")
-        nc.sync.dma_start(x_tile[:], x)
         offsets = held.tile([P, experts * piece], U16, name="offsets")
         nc.sync.dma_start(offsets[:], offs)
+        x_tile = held.tile([P, experts * entries], BF16, name="x_tile")
+        nc.sync.dma_start(x_tile[:], x)
+        w_tile = held.tile([P, experts, features], BF16, name="w_tile")
+        nc.sync.dma_start(w_tile[:], w.rearrange("e k m -> k e m"))
         gain = held.tile([P, blocks], F32, name="gain")
         nc.sync.dma_start(gain[:], s.rearrange("(a p) o -> p (a o)", p=P))
 

@@ -19,20 +19,22 @@ def tile_rows_placenorm_base_kernel(tc, base, x, w, s, offs, out):
     entries = x.shape[1] // experts
     piece = entries // 16
     half = tokens // 2
-    warmups = 3
+    warmups = 2
 
     with (
         tc.tile_pool(name="held", bufs=1) as held,
         tc.psum_pool(name="psum", bufs=1) as psum,
     ):
-        base_tile = held.tile([P, blocks, tokens], BF16, name="base_tile")
-        nc.sync.dma_start(base_tile[:], base.rearrange("(a p) n -> p a n", p=P))
+        base_tiles = [held.tile([P, tokens], BF16, name=f"base{a}") for a in range(blocks)]
+        for a in range(blocks):
+            nc.sync.dma_start(base_tiles[a][:], base[a * P : (a + 1) * P, :])
         offsets = held.tile([P, experts * piece], U16, name="offsets")
         nc.sync.dma_start(offsets[:], offs)
         x_tile = held.tile([P, experts * entries], BF16, name="x_tile")
         nc.sync.dma_start(x_tile[:], x)
-        w_tile = held.tile([P, experts, features], BF16, name="w_tile")
-        nc.sync.dma_start(w_tile[:], w.rearrange("e k m -> k e m"))
+        pairs = [held.tile([P, 2, features], BF16, name=f"pair{q}") for q in range(experts // 2)]
+        for q in range(experts // 2):
+            nc.sync.dma_start(pairs[q][:], w[2 * q : 2 * q + 2].rearrange("e k m -> k e m"))
         gain = held.tile([P, blocks], F32, name="gain")
         nc.sync.dma_start(gain[:], s.rearrange("(a p) o -> p (a o)", p=P))
 
@@ -54,13 +56,13 @@ def tile_rows_placenorm_base_kernel(tc, base, x, w, s, offs, out):
 
         windows = [psum.tile([P, tokens], F32, name=f"window{a}") for a in range(blocks)]
         for a in range(blocks):
-            nc.tensor.matmul(windows[a][:], identity[:], base_tile[:, a, :], start=True, stop=False)
+            nc.tensor.matmul(windows[a][:], identity[:], base_tiles[a][:], start=True, stop=False)
 
         for a in range(blocks):
             for e in range(experts):
                 nc.tensor.matmul(
                     windows[a][:].indirect(offsets[:, e * piece : (e + 1) * piece]),
-                    w_tile[:, e, a * P : (a + 1) * P],
+                    pairs[e // 2][:, e % 2, a * P : (a + 1) * P],
                     x_tile[:, e * entries : (e + 1) * entries],
                     start=False,
                     stop=e == experts - 1,

@@ -19,7 +19,7 @@ def tile_rows_placenorm_base_kernel(tc, base, x, w, s, offs, out):
     entries = x.shape[1] // experts
     piece = entries // 16
     half = tokens // 2
-    warmups = 2
+    warmups = 16
 
     with (
         tc.tile_pool(name="held", bufs=1) as held,
@@ -38,11 +38,11 @@ def tile_rows_placenorm_base_kernel(tc, base, x, w, s, offs, out):
         gain = held.tile([P, blocks], F32, name="gain")
         nc.sync.dma_start(gain[:], s.rearrange("(a p) o -> p (a o)", p=P))
 
-        zeros = held.tile([P, tokens], BF16, name="zeros")
+        zeros = held.tile([P, P], BF16, name="zeros")
         nc.vector.memset(zeros[:], 0.0)
-        spare = psum.tile([P, tokens], F32, name="spare")
+        spare = psum.tile([P, P], F32, name="spare")
         for warmup in range(warmups):
-            nc.tensor.matmul(spare[:], zeros[:, :P], zeros[:], start=True, stop=True)
+            nc.tensor.matmul(spare[:], zeros[:], zeros[:], start=True, stop=True)
 
         identity = held.tile([P, P], BF16, name="identity")
         make_identity(nc, identity[:])

import concourse.mybir as mybir
from concourse.masks import make_identity

BF16, F32, U16 = mybir.dt.bfloat16, mybir.dt.float32, mybir.dt.uint16
MULT = mybir.AluOpType.mult
ABS_RSQRT = mybir.ActivationFunctionType.Abs_reciprocal_sqrt
SQUARE = mybir.ActivationFunctionType.Square

P = 128
EPS = 1e-5
FLOPS = 2 * 128 * 384 * 512


def tile_rows_placenorm_base_kernel(tc, base, x, w, s, offs, out):
    nc = tc.nc
    features, tokens = base.shape
    experts = w.shape[0]
    blocks = features // P
    entries = x.shape[1] // experts
    piece = entries // 16
    half = tokens // 2
    warmups = 16

    with (
        tc.tile_pool(name="held", bufs=1) as held,
        tc.psum_pool(name="psum", bufs=1) as psum,
    ):
        base_tiles = [held.tile([P, tokens], BF16, name=f"base{a}") for a in range(blocks)]
        for a in range(blocks):
            nc.sync.dma_start(base_tiles[a][:], base[a * P : (a + 1) * P, :])
        offsets = held.tile([P, experts * piece], U16, name="offsets")
        nc.sync.dma_start(offsets[:], offs)
        x_tile = held.tile([P, experts * entries], BF16, name="x_tile")
        nc.sync.dma_start(x_tile[:], x)
        pairs = [held.tile([P, 2, features], BF16, name=f"pair{q}") for q in range(experts // 2)]
        for q in range(experts // 2):
            nc.sync.dma_start(pairs[q][:], w[2 * q : 2 * q + 2].rearrange("e k m -> k e m"))
        gain = held.tile([P, blocks], F32, name="gain")
        nc.sync.dma_start(gain[:], s.rearrange("(a p) o -> p (a o)", p=P))

        zeros = held.tile([P, P], BF16, name="zeros")
        nc.vector.memset(zeros[:], 0.0)
        spare = psum.tile([P, P], F32, name="spare")
        for warmup in range(warmups):
            nc.tensor.matmul(spare[:], zeros[:], zeros[:], start=True, stop=True)

        identity = held.tile([P, P], BF16, name="identity")
        make_identity(nc, identity[:])
        ones = held.tile([P, P], BF16, name="ones")
        nc.vector.memset(ones[:], 1.0)
        eps = held.tile([P, 1], F32, name="eps")
        nc.vector.memset(eps[:], EPS)

        early = held.tile([P, 1], F32, name="early")
        nc.scalar.activation(early[:], eps[:], ABS_RSQRT, bias=eps[:])

        windows = [psum.tile([P, tokens], F32, name=f"window{a}") for a in range(blocks)]
        for a in range(blocks):
            nc.tensor.matmul(windows[a][:], identity[:], base_tiles[a][:], start=True, stop=False)

        for a in range(blocks):
            for e in range(experts):
                nc.tensor.matmul(
                    windows[a][:].indirect(offsets[:, e * piece : (e + 1) * piece]),
                    pairs[e // 2][:, e % 2, a * P : (a + 1) * P],
                    x_tile[:, e * entries : (e + 1) * entries],
                    start=False,
                    stop=e == experts - 1,
                )

        squares = [held.tile([P, tokens], BF16, name=f"squares{a}") for a in range(blocks)]
        for a in range(blocks - 1):
            nc.scalar.activation(squares[a][:], windows[a][:], SQUARE)
        for h in range(2):
            cols = slice(h * half, (h + 1) * half)
            nc.scalar.activation(squares[-1][:, cols], windows[-1][:, cols], SQUARE)

        sums = [psum.tile([P, half], F32, name=f"sums{h}") for h in range(2)]
        for h in range(2):
            cols = slice(h * half, (h + 1) * half)
            for a in range(blocks):
                nc.tensor.matmul(sums[h][:], ones[:], squares[a][:, cols], start=a == 0, stop=a == blocks - 1)

        for h in range(2):
            cols = slice(h * half, (h + 1) * half)
            rnorm = held.tile([P, half], F32, name=f"rnorm{h}")
            nc.scalar.activation(rnorm[:], sums[h][:], ABS_RSQRT, bias=eps[:], scale=1.0 / features)
            for a in range(blocks):
                normed = held.tile([P, half], F32, name=f"normed{h}_{a}")
                nc.vector.scalar_tensor_tensor(
                    normed[:], windows[a][:, cols], gain[:, a : a + 1], rnorm[:], op0=MULT, op1=MULT
                )
                nc.sync.dma_start(out[a * P : (a + 1) * P, cols], normed[:])
